import numpy as np, ml_dtypes
CORES = [3,7,11,15,131,135,139,143]
N = 8
import mx_ref
BF = ml_dtypes.bfloat16
def cols(t, e):
    v = np.concatenate([t.reshape(128, -1, 4), np.zeros((128, 1, 4), BF)], axis=1)
    return np.ascontiguousarray(v[:, e]).reshape(128, -1)
def f(rng, *shape):
    return mx_ref.flush((rng.standard_normal(shape, dtype=np.float32) * np.exp2(rng.integers(-2, 3, shape[:-1] + (1,)))).astype(BF))
def wide(rng, *shape, cols=0):
    v = rng.standard_normal(shape, dtype=np.float32) * np.exp2(rng.integers(-12, 13, shape)).astype(np.float32)
    if cols: v *= np.repeat(np.exp2(rng.integers(-cols, cols + 1, shape[:-2] + (1, shape[-1] // 4))) * (rng.random(shape[:-2] + (1, shape[-1] // 4)) > 0.0625), 4, axis=-1).astype(np.float32)
    return mx_ref.flush(v.astype(BF))
T, NBIT, K, O = 96, 7, 128, 2
def planes(rng):
    v = np.zeros((N, 128, 512), BF); v[:, :, :4 * NBIT] = f(rng, N, 128, 4 * NBIT); return v
def setup_inputs(rng):
    return {"x": f(rng, N, 128, 4 * T), "hp": planes(rng), "e": f(rng, N, 128, 4 * K), "qw": f(rng, N, 128, O * 512)}
def setup_inputs_zero(rng):
    d = setup_inputs(rng)
    for r in rng.permutation(N)[:N // 2]:
        i = rng.integers(0, NBIT); d["hp"][r, :, 4 * i:4 * i + 4] = 0
    for r in range(N):
        for j in rng.permutation(T)[:T // 8]: d["x"][r, :, 4 * j:4 * j + 4] = 0
    return d
def setup_inputs_onebucket(rng):
    d = setup_inputs(rng); d["x"] = np.tile(d["hp"][rng.integers(0, N)][:, :4], (N, 1, T)); return d
def setup_inputs_all(rng):
    d = setup_inputs(rng); g = f(rng, 128, 4).astype(np.float32)[None, :, None, :]
    d["hp"][:, :, :4 * NBIT] = (g * np.exp2(rng.integers(0, 4, (N, 1, NBIT, 1)))).reshape(N, 128, -1).astype(BF)
    s = np.stack([rng.permutation(T) % 2 * 2 - 1 for r in range(N)]) * np.exp2(rng.integers(0, 4, (N, T)))
    d["x"] = (g * s[:, None, :, None]).reshape(N, 128, -1).astype(BF); return d
def setup_inputs_small(rng):
    d = setup_inputs(rng)
    for k in ("x", "hp"):
        v = d[k].astype(np.float32) * np.float32(2.0 ** -24)
        d[k] = mx_ref.flush(np.where(np.abs(v) < np.float32(2.0 ** -30), np.float32(0), v).astype(BF))
    return d
def setup_inputs_spread(rng):
    d = setup_inputs(rng); d["x"] = wide(rng, N, 128, 4 * T, cols=8); d["e"] = wide(rng, N, 128, 4 * K, cols=8); return d
def check_inputs(d):
    b = []
    if (np.asarray(d["hp"]).astype(np.float32)[:, :, 4 * NBIT:] != 0).any(): b.append("hp")
    return b
def reference(x, hp, e, qw):
    X = [mx_ref.quantize(x[r]) for r in range(N)]
    H = [mx_ref.quantize(hp[q]) for q in range(N)]
    W = [[mx_ref.quantize(np.ascontiguousarray(qw[r][:, 512 * o:512 * o + 512])) for o in range(O)] for r in range(N)]
    y = np.zeros((N, 128, N * O * T), np.float32); bk = np.zeros((N, N, T), np.float32)
    for r in range(N):
        for q in range(N):
            s = mx_ref.matmul(H[q], X[r])
            b = np.zeros(T, int)
            for i in range(NBIT): b += 2 ** i * (s[i] > 0)
            bk[r, q] = b
            c = mx_ref.quantize(cols(e[q], b))
            for o in range(O):
                k = (q * O + o) * T
                y[r][:, k:k + T] = mx_ref.matmul(W[r][o], c)
    return {"y": y, "bk": bk}

@@ -1,0 +1,301 @@
+import math
+from concourse.bass import DstId, RemoteDMATransfer
+from concourse.mybir import dt, AluOpType, ActivationFunctionType
+
+T_TOK, NBIT, K, O, N = 96, 7, 128, 2, 8
+G = 16
+A = T_TOK // G
+SL = 8
+RUN = K + SL
+NH = 128
+O0 = 8
+OP = O0 + RUN
+TP = OP + NH
+TA, HA = 0, K
+ZZ = HA + SL
+BASE = (O0 + SL, TP + RUN, TP + RUN + 2 * RUN + NH)
+ZEROS = (NH - SL, NH, NH - 2 * SL)
+HB = tuple(ZZ + z for z in ZEROS)
+TB = tuple(b + SL for b in HB)
+TO1 = BASE[2] + TB[2] + K
+TO2 = TO1 + K
+COLS = TO2 + K
+HBANKS, TBANKS = 4, 4
+HE = 8
+
+SCRATCH = {
+    "hb": ("sbuf", [128, 4 * (SL + NH)], "bfloat16"),
+    "eb": ("sbuf", [128, 4 * RUN], "bfloat16"),
+    "xs": ("sbuf", [128, A, 4 * G], "bfloat16"),
+    "xr": ("sbuf", [128, A, 512], "bfloat16"),
+    "qb": ("sbuf", [128, O * 512], "bfloat16"),
+    "ec": ("sbuf", [128, COLS], "float8_e4m3fn_x4"),
+    "es": ("sbuf", [128, COLS], "uint8"),
+    "xc": ("sbuf", [128, A * 128], "float8_e4m3fn_x4"),
+    "xp": ("sbuf", [128, A * 128], "uint8"),
+    "qc": ("sbuf", [128, O * 128], "float8_e4m3fn_x4"),
+    "qp": ("sbuf", [128, O * 128], "uint8"),
+    "bits": ("sbuf", [128, N * 64], "bfloat16"),
+    "half": ("sbuf", [128, 256], "bfloat16"),
+    "bsum": ("sbuf", [128, N * 64], "float32"),
+    "offs": ("sbuf", [128, N * 8], "uint16"),
+    "bt": ("sbuf", [128, 64], "float32"),
+    "prod": ("sbuf", [128, N * O * K], "float32"),
+    "ys": ("sbuf", [128, N * O * T_TOK], "float32"),
+    "hps": ("psum", [128, 512 * HBANKS], "float32"),
+    "tps": ("psum", [128, 512 * TBANKS], "float32"),
+}
+SEMAPHORES = ["le", "lh", "lx", "lq", "v", "s", "t", "ah", "hc", "hs", "ap", "a1c", "a1s", "a2", "a3", "z", "sent", "st", "sst"]
+
+
+def send(g, core, T, topo, items, n, codes):
+    tr = []
+    for d, es, c0, c1, s in items:
+        rid, pid = topo.addr(d, core)
+        buf = T.ec if codes else T.es
+        src, dst = buf[:, c0:c0 + n], buf[:, c1:c1 + n]
+        if codes:
+            src, dst = src.bitcast(dt.uint8), dst.bitcast(dt.uint8)
+        tr.append(RemoteDMATransfer(dst_ids=[DstId(rid=rid, pnc=pid)], dma_engine_mask=sum(1 << e for e in es), remote_sem=s, src=src, dst=dst))
+    g.remote_dma_fused(tr, local_sem=T.sem.sent)
+    return sum(len(i[1]) for i in items)
+
+
+def helper_program(g, core, dests, T, topo):
+    items = []
+    for d in dests:
+        es = topo.engines(core, d)
+        n = len(es) // 2
+        if topo.same_plane(core, d):
+            items.append((d, es[:n], 0, BASE[2] + ZZ, T.sem.ah))
+        else:
+            items.append((d, es[n:], 0, BASE[2] + ZZ + SL, T.sem.ah))
+    sent = 0
+    for codes, s in ((True, T.sem.hc), (False, T.sem.hs)):
+        g.wait_ge(s, HE)
+        sent += send(g, core, T, topo, items, SL, codes)
+    g.wait_ge(T.sem.sent, sent)
+
+
+def rank_program(g, core, T, topo):
+    sem = T.sem
+    helper = None
+    for r in T.cores:
+        if core not in topo.cores_of(r):
+            continue
+        dests = [d for d in T.cores if topo.die(d) != topo.die(r) and d not in topo.cores_of(r) and not topo.mates(r, d)]
+        spare = [c for c in topo.cores_of(r) if c not in T.cores and topo.die(c) == topo.die(r) and all(topo.may_write(c, d) for d in dests)]
+        if core == spare[0]:
+            helper_program(g, core, dests, T, topo)
+        if core == r:
+            helper = spare[0]
+    rank = T.rank_of(core)
+    if rank is None:
+        return
+    who = {"own": core}
+    for d in T.cores:
+        if d == core:
+            continue
+        same = topo.die(d) == topo.die(core)
+        if d in topo.cores_of(core):
+            who["partner"] = d
+        elif topo.mates(core, d):
+            who["mate_a" if same else "mate_b"] = d
+        elif topo.same_plane(core, d):
+            who["plane" if same else "plane_o"] = d
+        else:
+            who["diag" if same else "diag_o"] = d
+    q_of = {n: T.rank_of(d) for n, d in who.items()}
+
+    cnt = {"v": 0, "s": 0, "t": 0}
+
+    def inc(call, name):
+        call.then_inc(sem[name], 1)
+        cnt[name] += 1
+        return cnt[name]
+
+    V, S, PE, Y = g.vector, g.scalar, g.tensor, g.sync
+    COPY = ActivationFunctionType.Copy
+
+    S.dma_start(T.hb[:, 0:4 * SL], T.hp[:, 0:4 * SL]).then_inc(sem.lh, 16)
+    Y.dma_start(T.eb[:, 4 * SL:4 * RUN], T.e[:]).then_inc(sem.le, 16)
+    Y.dma_start(T.xs[:], T.x[:]).then_inc(sem.lx, 16)
+    Y.dma_start(T.qb[:], T.qw[:]).then_inc(sem.lq, 16)
+
+    inc(V.memset(T.hb[:, 4 * SL:4 * (SL + NH)], 0.0), "v")
+    m = inc(V.memset(T.half[:], 0.5), "v")
+    inc(V.memset(T.bits[:], 0.0), "v")
+    V.wait_ge(sem.v, m)
+    inc(V.memset(T.half[:, 0:256:8], 0.0), "v")
+    V.wait_ge(sem.v, cnt["v"])
+    V.wait_ge(sem.lh, 16)
+    hq = inc(V.quantize_mx(T.ec[:, OP:TP], T.es[:, OP:TP], T.hb[:, 0:4 * NH]), "v")
+    n = inc(V.tensor_copy(T.eb[:, 0:4 * SL], T.hb[:, 0:4 * SL]), "v")
+    V.wait_ge(sem.v, n)
+    V.wait_ge(sem.le, 16)
+    own = inc(V.quantize_mx(T.ec[:, O0:OP], T.es[:, O0:OP], T.eb[:]), "v")
+    z1 = BASE[1] + ZZ
+    inc(V.quantize_mx(T.ec[:, z1:z1 + NH], T.es[:, z1:z1 + NH], T.hb[:, 4 * SL:4 * (SL + NH)]), "v")
+
+    c0, c1, w = OP + SL, BASE[2] + ZZ + 2 * SL, ZEROS[2] - 2 * SL
+    Y.wait_ge(sem.v, hq)
+    Y.dma_start(T.ec[:, c1:c1 + w].bitcast(dt.uint8), T.ec[:, c0:c0 + w].bitcast(dt.uint8)).then_inc(sem.z, 16)
+    Y.dma_start(T.es[:, c1:c1 + w], T.es[:, c0:c0 + w]).then_inc(sem.z, 16)
+
+    far = topo.engines(core, who["diag"])
+    near = topo.engines(core, who["partner"])
+    inner = [e for e in near if e not in far]
+    h = len(far) // 2
+    hi = len(inner) // 2
+
+    def early(s):
+        return [(helper, inner[:HE], OP, 0, s)]
+
+    def first(s):
+        return [(who["plane"], far[:h], O0 + SL, BASE[1] + TA, s), (who["diag"], far[h:], O0, BASE[1] + HB[1], s),
+                (who["partner"], inner, O0, TP, sem.ap)]
+
+    second = [(who["mate_a"], far[:h], O0 + SL, BASE[2] + TA, sem.a2), (who["mate_b"], far[h:], O0, BASE[2] + HB[2], sem.a2)]
+
+    def relay(e1, e2):
+        return [(who["partner"], e1, BASE[1] + TA, TO1, sem.a3), (who["partner"], e2, BASE[1] + TB[1], TO2, sem.a3)]
+
+    def snd(items, n, codes):
+        return send(g, core, T, topo, items, n, codes)
+
+    g.wait_ge(sem.v, hq)
+    sent = snd(early(sem.hc), SL, True)
+    g.wait_ge(sem.v, own)
+    sent += snd(first(sem.a1c), RUN, True)
+    sent += snd(early(sem.hs), SL, False)
+    sent += snd(first(sem.a1s), RUN, False)
+    sent += snd(second, RUN, True)
+    sent += snd(second, RUN, False)
+    g.wait_ge(sem.a1c, len(far))
+    sent += snd(relay(inner[:hi], inner[hi:]), K, True)
+    g.wait_ge(sem.a1s, len(far))
+    sent += snd(relay(far, inner), K, False)
+
+    V.wait_ge(sem.lx, 16)
+    S.wait_ge(sem.lx, 16)
+    for i in range(8):
+        o_, i_ = T.xr[:, :, 4 * G * i:4 * G * (i + 1)], T.xs[:, :, :]
+        if i < 5:
+            vx = inc(V.tensor_copy(o_, i_), "v")
+        else:
+            sx = inc(S.activation(o_, i_, COPY), "s")
+    V.wait_ge(sem.v, vx)
+    V.wait_ge(sem.s, sx)
+    for a in range(A):
+        inc(V.quantize_mx(T.xc[:, 128 * a:128 * (a + 1)], T.xp[:, 128 * a:128 * (a + 1)], T.xr[:, a, :]), "v")
+    V.wait_ge(sem.lq, 16)
+    qq = inc(V.quantize_mx(T.qc[:], T.qp[:], T.qb[:]), "v")
+
+    hfree, tfree, nt = [0] * HBANKS, [None] * TBANKS, [0]
+
+    def hashes(p, runs):
+        c, nh = BASE[p] + HA, 2 * SL + ZEROS[p]
+        for a in range(A):
+            b = a % HBANKS
+            if hfree[b]:
+                PE.wait_ge(sem.v, hfree[b])
+            t = inc(PE.matmul_mx(T.hps[:, 512 * b:512 * b + nh], T.xc[:, 128 * a:128 * (a + 1)], T.xp[:, 128 * a:128 * (a + 1)],
+                                 T.ec[:, c:c + nh], T.es[:, c:c + nh], True, True), "t")
+            V.wait_ge(sem.t, t)
+            for c0, ks in runs:
+                w = SL * len(ks)
+                d, s = 64 * ks[0] + w * a, 512 * b + c0
+                hfree[b] = inc(V.tensor_scalar(T.bits[:, d:d + w - 1], T.hps[:, s:s + w - 1], 0.0, float(2 ** (NBIT - 1)),
+                                               AluOpType.is_gt, AluOpType.mult), "v")
+        ks = sorted(k for c0, l in runs for k in l)
+        lo, hi_ = 64 * ks[0], 64 * (ks[-1] + 1)
+        V.wait_ge(sem.v, cnt["v"])
+        n = inc(V.tensor_tensor_scan(T.bsum[:, lo:hi_], T.half[:, 0:hi_ - lo], T.bits[:, lo:hi_], 0.0, AluOpType.mult, AluOpType.add), "v")
+        V.wait_ge(sem.v, n)
+        if all(len(l) == 1 for c0, l in runs):
+            return inc(V.tensor_copy(T.offs[:, 8 * ks[0]:8 * (ks[-1] + 1)], T.bsum[:, lo + NBIT - 1:hi_:8]), "v")
+        for c0, l in runs:
+            w = SL * len(l)
+            for i, k in enumerate(l):
+                f = 64 * l[0] + SL * i + NBIT - 1
+                r = inc(V.tensor_copy(T.offs[:, 8 * k:8 * k + A], T.bsum[:, f:64 * l[0] + A * w:w]), "v")
+        return r
+
+    ready = {}
+
+    def tables(c, name, on_vector=False):
+        for o in range(O):
+            i = nt[0] % TBANKS
+            nt[0] += 1
+            if tfree[i]:
+                PE.wait_ge(*tfree[i])
+            t = inc(PE.matmul_mx(T.tps[:, 512 * i:512 * i + K], T.qc[:, 128 * o:128 * (o + 1)], T.qp[:, 128 * o:128 * (o + 1)],
+                                 T.ec[:, c:c + K], T.es[:, c:c + K], True, True), "t")
+            E, n = (V, "v") if on_vector else (S, "s")
+            E.wait_ge(sem.t, t)
+            w = (q_of[name] * O + o) * K
+            out, in_ = T.prod[:, w:w + K], T.tps[:, 512 * i:512 * i + K]
+            tfree[i] = ready[name] = (sem[n], inc(V.tensor_copy(out, in_) if on_vector else S.activation(out, in_, COPY), n))
+
+    nst = {"st": 0, "sst": 0}
+
+    def pick(name, k, lists, on_vector):
+        q = q_of[name]
+        E, D, own_, dsem = (V, Y, "v", "st") if on_vector else (S, S, "s", "sst")
+        E.wait_ge(sem.v, lists)
+        E.wait_ge(*ready[name])
+        for o in range(O):
+            j = q * O + o
+            out, win = T.ys[:, T_TOK * j:T_TOK * (j + 1)], T.prod[:, K * j:K * (j + 1)].indirect(T.offs[:, 8 * k:8 * k + A])
+            n = inc(V.tensor_copy(out, win) if on_vector else S.activation(out, win, COPY), own_)
+        w = O * T_TOK
+        D.wait_ge(sem[own_], n)
+        D.dma_start(T.y[:, w * q:w * (q + 1)], T.ys[:, w * q:w * (q + 1)]).then_inc(sem[dsem], 16)
+        nst[dsem] += 16
+
+    def buckets(b, rows):
+        n = inc(V.transpose(T.bt[0:32, 32 * b:32 * (b + 1)], T.bsum[0:32, 256 * b + NBIT - 1:256 * (b + 1):8]), "v")
+        Y.wait_ge(sem.v, n)
+        for name, p, step in rows:
+            q = q_of[name]
+            Y.dma_start(T.bk[q:q + 1, :], T.bt[p:p + (A - 1) * step + 1:step, 32 * b:32 * b + G]).then_inc(sem.st, 16)
+            nst["st"] += 16
+
+    PE.wait_ge(sem.v, qq)
+    tables(BASE[0] + TA, "own")
+    PE.wait_ge(sem.ap, 2 * len(inner))
+    l0 = hashes(0, [(0, [0]), (SL + ZEROS[0], [1])])
+    tables(TP + SL, "partner")
+    pick("own", 0, l0, False)
+    pick("partner", 1, l0, False)
+
+    PE.wait_ge(sem.a1c, len(far))
+    PE.wait_ge(sem.a1s, len(far))
+    l1 = hashes(1, [(0, [2]), (SL + ZEROS[1], [3])])
+    tables(BASE[1] + TA, "plane")
+    tables(BASE[1] + TB[1], "diag")
+    pick("plane", 2, l1, True)
+    pick("diag", 3, l1, False)
+    buckets(0, [("own", 0, 1), ("partner", 8, 1), ("plane", 16, 1), ("diag", 24, 1)])
+
+    PE.wait_ge(sem.a2, 2 * len(far))
+    PE.wait_ge(sem.ah, 2 * len(far))
+    PE.wait_ge(sem.z, 32)
+    l2 = hashes(2, [(0, [4, 5, 6]), (SL + ZEROS[2], [7])])
+    tables(BASE[2] + TA, "mate_a")
+    tables(BASE[2] + TB[2], "mate_b")
+    pick("mate_a", 4, l2, True)
+    PE.wait_ge(sem.a3, 2 * len(inner) + len(far))
+    tables(TO1, "plane_o", True)
+    pick("mate_b", 7, l2, False)
+    tables(TO2, "diag_o")
+    pick("plane_o", 5, l2, True)
+    pick("diag_o", 6, l2, False)
+    buckets(1, [("mate_a", 0, 3), ("plane_o", 1, 3), ("diag_o", 2, 3), ("mate_b", 24, 1)])
+
+    g.wait_ge(sem.sent, sent)
+    g.wait_ge(sem.v, cnt["v"])
+    g.wait_ge(sem.s, cnt["s"])
+    g.wait_ge(sem.t, cnt["t"])
+    S.wait_ge(sem.sst, nst["sst"])
+    Y.wait_ge(sem.st, nst["st"])

@@ -1,51 +1,54 @@
-import math
 from concourse.bass import DstId, RemoteDMATransfer
 from concourse.mybir import dt, AluOpType, ActivationFunctionType
 
 T_TOK, NBIT, K, O, N = 96, 7, 128, 2, 8
 G = 16
+B = 32
 A = T_TOK // G
 SL = 8
 RUN = K + SL
 NH = 128
+XW = A * B
 O0 = 8
 OP = O0 + RUN
 TP = OP + NH
-TA, HA = 0, K
-ZZ = HA + SL
-BASE = (O0 + SL, TP + RUN, TP + RUN + 2 * RUN + NH)
-ZEROS = (NH - SL, NH, NH - 2 * SL)
-HB = tuple(ZZ + z for z in ZEROS)
-TB = tuple(b + SL for b in HB)
-TO1 = BASE[2] + TB[2] + K
-TO2 = TO1 + K
-COLS = TO2 + K
-HBANKS, TBANKS = 4, 4
+Z1 = TP + RUN + 8
+P1 = Z1 + NH
+Z2 = P1 + 2 * RUN
+P2 = Z2 + NH
+HP = P2 + 2 * RUN
+Z3 = HP + 2 * SL
+P3 = Z3 + NH
+COLS = P3 + 2 * K
+HBANKS, TBANKS = 2, 6
 HE = 8
+LW = A * SL
+BW = 256
 
 SCRATCH = {
     "hb": ("sbuf", [128, 4 * (SL + NH)], "bfloat16"),
     "eb": ("sbuf", [128, 4 * RUN], "bfloat16"),
     "xs": ("sbuf", [128, A, 4 * G], "bfloat16"),
-    "xr": ("sbuf", [128, A, 512], "bfloat16"),
+    "xr": ("sbuf", [128, A, 4 * B], "bfloat16"),
     "qb": ("sbuf", [128, O * 512], "bfloat16"),
     "ec": ("sbuf", [128, COLS], "float8_e4m3fn_x4"),
     "es": ("sbuf", [128, COLS], "uint8"),
-    "xc": ("sbuf", [128, A * 128], "float8_e4m3fn_x4"),
-    "xp": ("sbuf", [128, A * 128], "uint8"),
+    "xc": ("sbuf", [128, XW], "float8_e4m3fn_x4"),
+    "xp": ("sbuf", [128, XW], "uint8"),
     "qc": ("sbuf", [128, O * 128], "float8_e4m3fn_x4"),
     "qp": ("sbuf", [128, O * 128], "uint8"),
-    "bits": ("sbuf", [128, N * 64], "bfloat16"),
-    "half": ("sbuf", [128, 256], "bfloat16"),
-    "bsum": ("sbuf", [128, N * 64], "float32"),
-    "offs": ("sbuf", [128, N * 8], "uint16"),
-    "bt": ("sbuf", [128, 64], "float32"),
+    "tr": ("sbuf", [128, A, B], "float32"),
+    "bits": ("sbuf", [128, 2 * BW], "bfloat16"),
+    "half": ("sbuf", [128, 4 * LW], "bfloat16"),
+    "bsum": ("sbuf", [128, 2 * BW], "float32"),
+    "offs": ("sbuf", [128, N * A], "uint16"),
+    "bt": ("sbuf", [128, 2 * B], "float32"),
     "prod": ("sbuf", [128, N * O * K], "float32"),
     "ys": ("sbuf", [128, N * O * T_TOK], "float32"),
     "hps": ("psum", [128, 512 * HBANKS], "float32"),
     "tps": ("psum", [128, 512 * TBANKS], "float32"),
 }
-SEMAPHORES = ["le", "lh", "lx", "lq", "v", "s", "t", "ah", "hc", "hs", "ap", "a1c", "a1s", "a2", "a3", "z", "sent", "st", "sst"]
+SEMAPHORES = ["le", "lh", "lx", "lq", "v", "s", "t", "ah", "hc", "hs", "ap", "a1c", "a1s", "a2", "a3", "sent", "st", "sst"]
 
 
 def send(g, core, T, topo, items, n, codes):
@@ -67,9 +70,9 @@ def helper_program(g, core, dests, T, topo):
         es = topo.engines(core, d)
         n = len(es) // 2
         if topo.same_plane(core, d):
-            items.append((d, es[:n], 0, BASE[2] + ZZ, T.sem.ah))
+            items.append((d, es[:n], 0, HP, T.sem.ah))
         else:
-            items.append((d, es[n:], 0, BASE[2] + ZZ + SL, T.sem.ah))
+            items.append((d, es[n:], 0, HP + SL, T.sem.ah))
     sent = 0
     for codes, s in ((True, T.sem.hc), (False, T.sem.hs)):
         g.wait_ge(s, HE)
@@ -106,6 +109,8 @@ def rank_program(g, core, T, topo):
         else:
             who["diag" if same else "diag_o"] = d
     q_of = {n: T.rank_of(d) for n, d in who.items()}
+    twos = [sorted(p, key=lambda n: q_of[n]) for p in (("own", "partner"), ("plane", "diag"), ("mate_a", "mate_b"), ("plane_o", "diag_o"))]
+    slot = {n: 2 * i + j for i, p in enumerate(twos) for j, n in enumerate(p)}
 
     cnt = {"v": 0, "s": 0, "t": 0}
 
@@ -123,10 +128,12 @@ def rank_program(g, core, T, topo):
     Y.dma_start(T.qb[:], T.qw[:]).then_inc(sem.lq, 16)
 
     inc(V.memset(T.hb[:, 4 * SL:4 * (SL + NH)], 0.0), "v")
-    m = inc(V.memset(T.half[:], 0.5), "v")
-    inc(V.memset(T.bits[:], 0.0), "v")
+    m = inc(V.memset(T.half[0:B, :], 0.5), "v")
+    for b in range(2):
+        inc(V.memset(T.bsum[0:B, BW * b + 4 * LW:BW * (b + 1)], 0.0), "v")
     V.wait_ge(sem.v, m)
-    inc(V.memset(T.half[:, 0:256:8], 0.0), "v")
+    inc(V.memset(T.half[0:B, 0:4 * LW:SL], 0.0), "v")
+
     V.wait_ge(sem.v, cnt["v"])
     V.wait_ge(sem.lh, 16)
     hq = inc(V.quantize_mx(T.ec[:, OP:TP], T.es[:, OP:TP], T.hb[:, 0:4 * NH]), "v")
@@ -134,31 +141,21 @@ def rank_program(g, core, T, topo):
     V.wait_ge(sem.v, n)
     V.wait_ge(sem.le, 16)
     own = inc(V.quantize_mx(T.ec[:, O0:OP], T.es[:, O0:OP], T.eb[:]), "v")
-    z1 = BASE[1] + ZZ
-    inc(V.quantize_mx(T.ec[:, z1:z1 + NH], T.es[:, z1:z1 + NH], T.hb[:, 4 * SL:4 * (SL + NH)]), "v")
-
-    c0, c1, w = OP + SL, BASE[2] + ZZ + 2 * SL, ZEROS[2] - 2 * SL
-    Y.wait_ge(sem.v, hq)
-    Y.dma_start(T.ec[:, c1:c1 + w].bitcast(dt.uint8), T.ec[:, c0:c0 + w].bitcast(dt.uint8)).then_inc(sem.z, 16)
-    Y.dma_start(T.es[:, c1:c1 + w], T.es[:, c0:c0 + w]).then_inc(sem.z, 16)
 
     far = topo.engines(core, who["diag"])
     near = topo.engines(core, who["partner"])
     inner = [e for e in near if e not in far]
     h = len(far) // 2
-    hi = len(inner) // 2
+    LEAD, TRAIL = O0, O0 + SL
 
     def early(s):
         return [(helper, inner[:HE], OP, 0, s)]
 
     def first(s):
-        return [(who["plane"], far[:h], O0 + SL, BASE[1] + TA, s), (who["diag"], far[h:], O0, BASE[1] + HB[1], s),
-                (who["partner"], inner, O0, TP, sem.ap)]
+        return [(who["plane"], far[:h], LEAD, P1, s), (who["diag"], far[h:], TRAIL, P1 + RUN, s), (who["partner"], inner, LEAD, TP, sem.ap)]
 
-    second = [(who["mate_a"], far[:h], O0 + SL, BASE[2] + TA, sem.a2), (who["mate_b"], far[h:], O0, BASE[2] + HB[2], sem.a2)]
-
-    def relay(e1, e2):
-        return [(who["partner"], e1, BASE[1] + TA, TO1, sem.a3), (who["partner"], e2, BASE[1] + TB[1], TO2, sem.a3)]
+    second = [(who["mate_a"], far[:h], LEAD, P2, sem.a2), (who["mate_b"], far[h:], TRAIL, P2 + RUN, sem.a2)]
+    relay = [(who["partner"], inner, P1 + SL, P3, sem.a3)]
 
     def snd(items, n, codes):
         return send(g, core, T, topo, items, n, codes)
@@ -172,126 +169,133 @@ def rank_program(g, core, T, topo):
     sent += snd(second, RUN, True)
     sent += snd(second, RUN, False)
     g.wait_ge(sem.a1c, len(far))
-    sent += snd(relay(inner[:hi], inner[hi:]), K, True)
+    sent += snd(relay, 2 * K, True)
     g.wait_ge(sem.a1s, len(far))
-    sent += snd(relay(far, inner), K, False)
+    sent += snd(relay, 2 * K, False)
 
     V.wait_ge(sem.lx, 16)
     S.wait_ge(sem.lx, 16)
-    for i in range(8):
-        o_, i_ = T.xr[:, :, 4 * G * i:4 * G * (i + 1)], T.xs[:, :, :]
-        if i < 5:
-            vx = inc(V.tensor_copy(o_, i_), "v")
-        else:
-            sx = inc(S.activation(o_, i_, COPY), "s")
-    V.wait_ge(sem.v, vx)
-    V.wait_ge(sem.s, sx)
-    for a in range(A):
-        inc(V.quantize_mx(T.xc[:, 128 * a:128 * (a + 1)], T.xp[:, 128 * a:128 * (a + 1)], T.xr[:, a, :]), "v")
+    vx = inc(V.tensor_copy(T.xr[:, :, 0:4 * G], T.xs[:, :, :]), "v")
+    sx = inc(S.activation(T.xr[:, :, 4 * G:4 * B], T.xs[:, :, :], COPY), "s")
     V.wait_ge(sem.lq, 16)
     qq = inc(V.quantize_mx(T.qc[:], T.qp[:], T.qb[:]), "v")
+    V.wait_ge(sem.v, vx)
+    V.wait_ge(sem.s, sx)
+    xq = inc(V.quantize_mx(T.xc[:], T.xp[:], T.xr[:, :, :]), "v")
+    for c in (Z1, Z2, Z3):
+        zq = inc(V.quantize_mx(T.ec[:, c:c + NH], T.es[:, c:c + NH], T.hb[:, 4 * SL:4 * (SL + NH)]), "v")
 
-    hfree, tfree, nt = [0] * HBANKS, [None] * TBANKS, [0]
+    hfree, tfree, nt, nh, trfree = [0] * HBANKS, [None] * TBANKS, [0], [0], [0]
 
-    def hashes(p, runs):
-        c, nh = BASE[p] + HA, 2 * SL + ZEROS[p]
-        for a in range(A):
-            b = a % HBANKS
-            if hfree[b]:
-                PE.wait_ge(sem.v, hfree[b])
-            t = inc(PE.matmul_mx(T.hps[:, 512 * b:512 * b + nh], T.xc[:, 128 * a:128 * (a + 1)], T.xp[:, 128 * a:128 * (a + 1)],
-                                 T.ec[:, c:c + nh], T.es[:, c:c + nh], True, True), "t")
-            V.wait_ge(sem.t, t)
-            for c0, ks in runs:
-                w = SL * len(ks)
-                d, s = 64 * ks[0] + w * a, 512 * b + c0
-                hfree[b] = inc(V.tensor_scalar(T.bits[:, d:d + w - 1], T.hps[:, s:s + w - 1], 0.0, float(2 ** (NBIT - 1)),
-                                               AluOpType.is_gt, AluOpType.mult), "v")
-        ks = sorted(k for c0, l in runs for k in l)
-        lo, hi_ = 64 * ks[0], 64 * (ks[-1] + 1)
-        V.wait_ge(sem.v, cnt["v"])
-        n = inc(V.tensor_tensor_scan(T.bsum[:, lo:hi_], T.half[:, 0:hi_ - lo], T.bits[:, lo:hi_], 0.0, AluOpType.mult, AluOpType.add), "v")
+    def planes(c, start, stop):
+        b = nh[0] % HBANKS
+        if start and hfree[b]:
+            PE.wait_ge(sem.v, hfree[b])
+        return inc(PE.matmul_mx(T.hps[:, 512 * b:512 * b + XW], T.ec[:, c:c + NH], T.es[:, c:c + NH], T.xc[:], T.xp[:], start, stop), "t")
+
+    def at(k):
+        return BW * (k // 4) + LW * (k % 4)
+
+    def lists(t, rows):
+        b = nh[0] % HBANKS
+        nh[0] += 1
+        V.wait_ge(sem.t, t)
+        n = hfree[b] = inc(V.transpose(T.tr[:, :, :], T.hps[:, 512 * b:512 * b + XW]), "v")
         V.wait_ge(sem.v, n)
-        if all(len(l) == 1 for c0, l in runs):
-            return inc(V.tensor_copy(T.offs[:, 8 * ks[0]:8 * (ks[-1] + 1)], T.bsum[:, lo + NBIT - 1:hi_:8]), "v")
-        for c0, l in runs:
-            w = SL * len(l)
-            for i, k in enumerate(l):
-                f = 64 * l[0] + SL * i + NBIT - 1
-                r = inc(V.tensor_copy(T.offs[:, 8 * k:8 * k + A], T.bsum[:, f:64 * l[0] + A * w:w]), "v")
-        return r
+        for name, row in rows.items():
+            p, i, d = row // B * B, row % B, at(slot[name])
+            n = inc(V.tensor_scalar(T.bits[0:B, d:d + LW], T.tr[p:p + B, :, i:i + SL], 0.0, float(2 ** (NBIT - 1)),
+                                    AluOpType.is_gt, AluOpType.mult), "v")
+        ks = sorted(slot[name] for name in rows)
+        lo, w = at(ks[0]), LW * len(ks)
+        V.wait_ge(sem.v, n)
+        n = inc(V.tensor_tensor_scan(T.bsum[0:B, lo:lo + w], T.half[0:B, 0:w], T.bits[0:B, lo:lo + w], 0.0, AluOpType.mult, AluOpType.add), "v")
+        V.wait_ge(sem.v, n)
+        for p in range(0, 128, B):
+            n = inc(V.tensor_copy(T.offs[p:p + B, A * ks[0]:A * (ks[-1] + 1)], T.bsum[0:B, lo + NBIT - 1:lo + w:SL]), "v")
+        return n
 
-    ready = {}
+    ready, where, used = {}, {}, [0]
 
-    def tables(c, name, on_vector=False):
+    def tables(c, names):
+        w = K * len(names)
         for o in range(O):
             i = nt[0] % TBANKS
             nt[0] += 1
             if tfree[i]:
-                PE.wait_ge(*tfree[i])
-            t = inc(PE.matmul_mx(T.tps[:, 512 * i:512 * i + K], T.qc[:, 128 * o:128 * (o + 1)], T.qp[:, 128 * o:128 * (o + 1)],
-                                 T.ec[:, c:c + K], T.es[:, c:c + K], True, True), "t")
-            E, n = (V, "v") if on_vector else (S, "s")
-            E.wait_ge(sem.t, t)
-            w = (q_of[name] * O + o) * K
-            out, in_ = T.prod[:, w:w + K], T.tps[:, 512 * i:512 * i + K]
-            tfree[i] = ready[name] = (sem[n], inc(V.tensor_copy(out, in_) if on_vector else S.activation(out, in_, COPY), n))
+                PE.wait_ge(sem.s, tfree[i])
+            t = inc(PE.matmul_mx(T.tps[:, 512 * i:512 * i + w], T.qc[:, 128 * o:128 * (o + 1)], T.qp[:, 128 * o:128 * (o + 1)],
+                                 T.ec[:, c:c + w], T.es[:, c:c + w], True, True), "t")
+            S.wait_ge(sem.t, t)
+            tfree[i] = inc(S.activation(T.prod[:, used[0]:used[0] + w], T.tps[:, 512 * i:512 * i + w], COPY), "s")
+            for j, name in enumerate(names):
+                ready[name, o], where[name, o] = tfree[i], used[0] + K * j
+            used[0] += w
 
     nst = {"st": 0, "sst": 0}
+    picked = {}
 
-    def pick(name, k, lists, on_vector):
-        q = q_of[name]
-        E, D, own_, dsem = (V, Y, "v", "st") if on_vector else (S, S, "s", "sst")
-        E.wait_ge(sem.v, lists)
-        E.wait_ge(*ready[name])
-        for o in range(O):
-            j = q * O + o
-            out, win = T.ys[:, T_TOK * j:T_TOK * (j + 1)], T.prod[:, K * j:K * (j + 1)].indirect(T.offs[:, 8 * k:8 * k + A])
-            n = inc(V.tensor_copy(out, win) if on_vector else S.activation(out, win, COPY), own_)
+    def pick(names, o, made):
+        E = S if o else V
+        E.wait_ge(sem.v, made)
+        E.wait_ge(sem.s, max(ready[name, o] for name in names))
+        for name in names:
+            j, c, k = q_of[name] * O + o, where[name, o], slot[name]
+            out, win = T.ys[:, T_TOK * j:T_TOK * (j + 1)], T.prod[:, c:c + K].indirect(T.offs[:, A * k:A * (k + 1)])
+            picked[name, o] = inc(S.activation(out, win, COPY), "s") if o else inc(V.tensor_copy(out, win), "v")
+
+    def store(names):
         w = O * T_TOK
-        D.wait_ge(sem[own_], n)
-        D.dma_start(T.y[:, w * q:w * (q + 1)], T.ys[:, w * q:w * (q + 1)]).then_inc(sem[dsem], 16)
-        nst[dsem] += 16
-
-    def buckets(b, rows):
-        n = inc(V.transpose(T.bt[0:32, 32 * b:32 * (b + 1)], T.bsum[0:32, 256 * b + NBIT - 1:256 * (b + 1):8]), "v")
-        Y.wait_ge(sem.v, n)
-        for name, p, step in rows:
+        for name in names:
             q = q_of[name]
-            Y.dma_start(T.bk[q:q + 1, :], T.bt[p:p + (A - 1) * step + 1:step, 32 * b:32 * b + G]).then_inc(sem.st, 16)
+            Y.wait_ge(sem.v, picked[name, 0])
+            Y.wait_ge(sem.s, picked[name, 1])
+            Y.dma_start(T.y[:, w * q:w * (q + 1)], T.ys[:, w * q:w * (q + 1)]).then_inc(sem.st, 16)
             nst["st"] += 16
 
-    PE.wait_ge(sem.v, qq)
-    tables(BASE[0] + TA, "own")
-    PE.wait_ge(sem.ap, 2 * len(inner))
-    l0 = hashes(0, [(0, [0]), (SL + ZEROS[0], [1])])
-    tables(TP + SL, "partner")
-    pick("own", 0, l0, False)
-    pick("partner", 1, l0, False)
+    def buckets(b, D, dsem):
+        n = inc(V.transpose(T.bt[0:B, B * b:B * (b + 1)], T.bsum[0:B, BW * b + NBIT - 1:BW * (b + 1):SL]), "v")
+        D.wait_ge(sem.v, n)
+        for i in range(2):
+            q0, q1 = (q_of[name] for name in twos[2 * b + i])
+            D.dma_start(T.bk[q0:q1 + 1:q1 - q0, :], T.bt[2 * A * i:2 * A * (i + 1), B * b:B * b + G]).then_inc(sem[dsem], 16)
+            nst[dsem] += 16
 
+    BEFORE = SL - NH
+    PE.wait_ge(sem.v, qq)
+    tables(TRAIL, ["own"])
+    PE.wait_ge(sem.v, xq)
+    planes(OP, True, False)
+    PE.wait_ge(sem.ap, 2 * len(inner))
+    l0 = lists(planes(TP + BEFORE, False, True), {"own": 0, "partner": NH - SL})
+    tables(TP + SL, ["partner"])
+    for o in range(O):
+        pick(["own", "partner"], o, l0)
+    store(["own", "partner"])
+
+    PE.wait_ge(sem.v, zq)
     PE.wait_ge(sem.a1c, len(far))
     PE.wait_ge(sem.a1s, len(far))
-    l1 = hashes(1, [(0, [2]), (SL + ZEROS[1], [3])])
-    tables(BASE[1] + TA, "plane")
-    tables(BASE[1] + TB[1], "diag")
-    pick("plane", 2, l1, True)
-    pick("diag", 3, l1, False)
-    buckets(0, [("own", 0, 1), ("partner", 8, 1), ("plane", 16, 1), ("diag", 24, 1)])
+    planes(P1 + BEFORE, True, False)
+    l1 = lists(planes(Z2 - SL, False, True), {"plane": NH - SL, "diag": 0})
+    tables(P1 + SL, ["plane", "diag"])
+    for o in range(O):
+        pick(["plane", "diag"], o, l1)
+    store(["plane", "diag"])
+    buckets(0, Y, "st")
 
     PE.wait_ge(sem.a2, 2 * len(far))
     PE.wait_ge(sem.ah, 2 * len(far))
-    PE.wait_ge(sem.z, 32)
-    l2 = hashes(2, [(0, [4, 5, 6]), (SL + ZEROS[2], [7])])
-    tables(BASE[2] + TA, "mate_a")
-    tables(BASE[2] + TB[2], "mate_b")
-    pick("mate_a", 4, l2, True)
-    PE.wait_ge(sem.a3, 2 * len(inner) + len(far))
-    tables(TO1, "plane_o", True)
-    pick("mate_b", 7, l2, False)
-    tables(TO2, "diag_o")
-    pick("plane_o", 5, l2, True)
-    pick("diag_o", 6, l2, False)
-    buckets(1, [("mate_a", 0, 3), ("plane_o", 1, 3), ("diag_o", 2, 3), ("mate_b", 24, 1)])
+    planes(P2 + BEFORE, True, False)
+    l2 = lists(planes(HP - SL, False, True), {"mate_a": NH - SL, "mate_b": 0, "plane_o": SL, "diag_o": 2 * SL})
+    tables(P2 + SL, ["mate_a", "mate_b"])
+    PE.wait_ge(sem.a3, 2 * len(inner))
+    tables(P3, ["plane_o", "diag_o"])
+    pick(["mate_a", "mate_b"], 0, l2)
+    pick(["plane_o", "diag_o"], 0, l2)
+    pick(["mate_a", "mate_b", "plane_o", "diag_o"], 1, l2)
+    store(["mate_a", "mate_b", "plane_o", "diag_o"])
+    buckets(1, S, "sst")
 
     g.wait_ge(sem.sent, sent)
     g.wait_ge(sem.v, cnt["v"])

@@ -9,10 +9,10 @@ SL = 8
 RUN = K + SL
 NH = 128
 XW = A * B
-O0 = 8
-OP = O0 + RUN
+OT = NH
+OP = OT + K
 TP = OP + NH
-Z1 = TP + RUN + 8
+Z1 = TP + RUN + SL
 P1 = Z1 + NH
 Z2 = P1 + 2 * RUN
 P2 = Z2 + NH
@@ -20,14 +20,15 @@ HP = P2 + 2 * RUN
 Z3 = HP + 2 * SL
 P3 = Z3 + NH
 COLS = P3 + 2 * K
+SRC = (OT - SL, OT)
+PL = (OT - SL, OP)
 HBANKS, TBANKS = 2, 6
-HE = 8
 LW = A * SL
-BW = 256
+BW = B * SL
 
 SCRATCH = {
-    "hb": ("sbuf", [128, 4 * (SL + NH)], "bfloat16"),
-    "eb": ("sbuf", [128, 4 * RUN], "bfloat16"),
+    "hb": ("sbuf", [128, 4 * (2 * NH + SL)], "bfloat16"),
+    "eb": ("sbuf", [128, 4 * K], "bfloat16"),
     "xs": ("sbuf", [128, A, 4 * G], "bfloat16"),
     "xr": ("sbuf", [128, A, 4 * B], "bfloat16"),
     "qb": ("sbuf", [128, O * 512], "bfloat16"),
@@ -37,64 +38,21 @@ SCRATCH = {
     "xp": ("sbuf", [128, XW], "uint8"),
     "qc": ("sbuf", [128, O * 128], "float8_e4m3fn_x4"),
     "qp": ("sbuf", [128, O * 128], "uint8"),
-    "tr": ("sbuf", [128, A, B], "float32"),
+    "tr": ("sbuf", [128, HBANKS * A, B], "float32"),
     "bits": ("sbuf", [128, 2 * BW], "bfloat16"),
-    "half": ("sbuf", [128, 4 * LW], "bfloat16"),
+    "half": ("sbuf", [128, BW], "bfloat16"),
     "bsum": ("sbuf", [128, 2 * BW], "float32"),
-    "offs": ("sbuf", [128, N * A], "uint16"),
+    "offs": ("sbuf", [128, 2 * B], "uint16"),
     "bt": ("sbuf", [128, 2 * B], "float32"),
     "prod": ("sbuf", [128, N * O * K], "float32"),
     "ys": ("sbuf", [128, N * O * T_TOK], "float32"),
     "hps": ("psum", [128, 512 * HBANKS], "float32"),
     "tps": ("psum", [128, 512 * TBANKS], "float32"),
 }
-SEMAPHORES = ["le", "lh", "lx", "lq", "v", "s", "t", "ah", "hc", "hs", "ap", "a1c", "a1s", "a2", "a3", "sent", "st", "sst"]
+SEMAPHORES = ["le", "lh", "lx", "lq", "v", "s", "t", "ah", "hc", "hs", "ap", "a0c", "a1c", "a0s", "a1s", "a2", "a3", "sent", "st", "sst"]
 
 
-def send(g, core, T, topo, items, n, codes):
-    tr = []
-    for d, es, c0, c1, s in items:
-        rid, pid = topo.addr(d, core)
-        buf = T.ec if codes else T.es
-        src, dst = buf[:, c0:c0 + n], buf[:, c1:c1 + n]
-        if codes:
-            src, dst = src.bitcast(dt.uint8), dst.bitcast(dt.uint8)
-        tr.append(RemoteDMATransfer(dst_ids=[DstId(rid=rid, pnc=pid)], dma_engine_mask=sum(1 << e for e in es), remote_sem=s, src=src, dst=dst))
-    g.remote_dma_fused(tr, local_sem=T.sem.sent)
-    return sum(len(i[1]) for i in items)
-
-
-def helper_program(g, core, dests, T, topo):
-    items = []
-    for d in dests:
-        es = topo.engines(core, d)
-        n = len(es) // 2
-        if topo.same_plane(core, d):
-            items.append((d, es[:n], 0, HP, T.sem.ah))
-        else:
-            items.append((d, es[n:], 0, HP + SL, T.sem.ah))
-    sent = 0
-    for codes, s in ((True, T.sem.hc), (False, T.sem.hs)):
-        g.wait_ge(s, HE)
-        sent += send(g, core, T, topo, items, SL, codes)
-    g.wait_ge(T.sem.sent, sent)
-
-
-def rank_program(g, core, T, topo):
-    sem = T.sem
-    helper = None
-    for r in T.cores:
-        if core not in topo.cores_of(r):
-            continue
-        dests = [d for d in T.cores if topo.die(d) != topo.die(r) and d not in topo.cores_of(r) and not topo.mates(r, d)]
-        spare = [c for c in topo.cores_of(r) if c not in T.cores and topo.die(c) == topo.die(r) and all(topo.may_write(c, d) for d in dests)]
-        if core == spare[0]:
-            helper_program(g, core, dests, T, topo)
-        if core == r:
-            helper = spare[0]
-    rank = T.rank_of(core)
-    if rank is None:
-        return
+def roles(core, T, topo):
     who = {"own": core}
     for d in T.cores:
         if d == core:
@@ -108,9 +66,76 @@ def rank_program(g, core, T, topo):
             who["plane" if same else "plane_o"] = d
         else:
             who["diag" if same else "diag_o"] = d
+    return who
+
+
+def transfer(core, T, topo, item, n, codes):
+    d, es, c0, c1, s = item
+    rid, pid = topo.addr(d, core)
+    buf = T.ec if codes else T.es
+    src, dst = buf[:, c0:c0 + n], buf[:, c1:c1 + n]
+    if codes:
+        src, dst = src.bitcast(dt.uint8), dst.bitcast(dt.uint8)
+    return RemoteDMATransfer(dst_ids=[DstId(rid=rid, pnc=pid)], dma_engine_mask=sum(1 << e for e in es), remote_sem=s, src=src, dst=dst)
+
+
+def send(g, core, T, topo, items, n, codes):
+    g.remote_dma_fused([transfer(core, T, topo, i, n, codes) for i in items], local_sem=T.sem.sent)
+    return sum(len(i[1]) for i in items)
+
+
+def halves(core, dests, c0, cols, s, topo):
+    items = []
+    for i, (d, c1) in enumerate(zip(dests, cols)):
+        es = topo.engines(core, d)
+        n = len(es) // 2
+        items.append((d, es[n * i:n * (i + 1)], c0, c1, s))
+    return items
+
+
+def inner_engines(core, who, topo):
+    far = topo.engines(core, who["diag"])
+    return [e for e in topo.engines(core, who["partner"]) if e not in far]
+
+
+def helper_program(g, core, r, T, topo):
+    who, side = roles(r, T, topo), topo.die(r)
+    codes, planes = ([(who["diag_o"], topo.engines(core, who["diag_o"]), c, HP + SL, T.sem.ah)] for c in (HP, PL[side]))
+    mates = halves(core, [who["mate_a"], who["mate_b"]], SRC[side], [P2 + RUN * side] * 2, T.sem.a2, topo)
+    n = len(inner_engines(r, who, topo))
+    g.wait_ge(T.sem.hc, n)
+    sent = send(g, core, T, topo, codes, SL, True)
+    g.wait_ge(T.sem.hs, n // 2)
+    sent += send(g, core, T, topo, planes, SL, False)
+    sent += send(g, core, T, topo, mates, RUN, False)
+    g.wait_ge(T.sem.sent, sent)
+
+
+def rank_program(g, core, T, topo):
+    sem = T.sem
+    helper = None
+    for r in T.cores:
+        if core not in topo.cores_of(r):
+            continue
+        dests = [d for d in T.cores if d not in topo.cores_of(r)]
+        spare = [c for c in topo.cores_of(r) if c not in T.cores and topo.die(c) == topo.die(r) and all(topo.may_write(c, d) for d in dests)]
+        if core == spare[0]:
+            helper_program(g, core, r, T, topo)
+        if core == r:
+            helper = spare[0]
+    rank = T.rank_of(core)
+    if rank is None:
+        return
+    who, side = roles(core, T, topo), topo.die(core)
     q_of = {n: T.rank_of(d) for n, d in who.items()}
-    twos = [sorted(p, key=lambda n: q_of[n]) for p in (("own", "partner"), ("plane", "diag"), ("mate_a", "mate_b"), ("plane_o", "diag_o"))]
-    slot = {n: 2 * i + j for i, p in enumerate(twos) for j, n in enumerate(p)}
+    early = ["own", "partner", "plane"]
+    late = sorted((n for n in who if n not in early), key=lambda n: q_of[n])
+    at = {n: BW * b + LW * k for b, names in enumerate((early, late)) for k, n in enumerate(names)}
+
+    def by_side(same, other):
+        return [other, same] if side else [same, other]
+
+    pair1, pair2, pair3 = by_side("plane", "diag"), by_side("mate_a", "mate_b"), by_side("diag_o", "plane_o")
 
     cnt = {"v": 0, "s": 0, "t": 0}
 
@@ -122,97 +147,107 @@ def rank_program(g, core, T, topo):
     V, S, PE, Y = g.vector, g.scalar, g.tensor, g.sync
     COPY = ActivationFunctionType.Copy
 
-    S.dma_start(T.hb[:, 0:4 * SL], T.hp[:, 0:4 * SL]).then_inc(sem.lh, 16)
-    Y.dma_start(T.eb[:, 4 * SL:4 * RUN], T.e[:]).then_inc(sem.le, 16)
+    S.dma_start(T.hb[:, 4 * NH:4 * (NH + SL)], T.hp[:, 0:4 * SL]).then_inc(sem.lh, 16)
+    Y.dma_start(T.eb[:], T.e[:]).then_inc(sem.le, 16)
     Y.dma_start(T.xs[:], T.x[:]).then_inc(sem.lx, 16)
     Y.dma_start(T.qb[:], T.qw[:]).then_inc(sem.lq, 16)
 
-    inc(V.memset(T.hb[:, 4 * SL:4 * (SL + NH)], 0.0), "v")
+    z = inc(V.memset(T.hb[:, 0:4 * NH], 0.0), "v")
+    inc(V.memset(T.hb[:, 4 * (NH + SL):], 0.0), "v")
     m = inc(V.memset(T.half[0:B, :], 0.5), "v")
-    for b in range(2):
-        inc(V.memset(T.bsum[0:B, BW * b + 4 * LW:BW * (b + 1)], 0.0), "v")
+    V.wait_ge(sem.v, z)
+    for c in (Z1, Z2):
+        inc(V.quantize_mx(T.ec[:, c:c + NH], T.es[:, c:c + NH], T.hb[:, 0:4 * NH]), "v")
     V.wait_ge(sem.v, m)
-    inc(V.memset(T.half[0:B, 0:4 * LW:SL], 0.0), "v")
+    inc(V.memset(T.half[0:B, 0:BW:SL], 0.0), "v")
 
-    V.wait_ge(sem.v, cnt["v"])
     V.wait_ge(sem.lh, 16)
-    hq = inc(V.quantize_mx(T.ec[:, OP:TP], T.es[:, OP:TP], T.hb[:, 0:4 * NH]), "v")
-    n = inc(V.tensor_copy(T.eb[:, 0:4 * SL], T.hb[:, 0:4 * SL]), "v")
-    V.wait_ge(sem.v, n)
+    hq = {}
+    for s in (side, 1 - side):
+        c, h = (OP, 4 * NH) if s else (0, 4 * SL)
+        hq[s] = inc(V.quantize_mx(T.ec[:, c:c + NH], T.es[:, c:c + NH], T.hb[:, h:h + 4 * NH]), "v")
     V.wait_ge(sem.le, 16)
-    own = inc(V.quantize_mx(T.ec[:, O0:OP], T.es[:, O0:OP], T.eb[:]), "v")
+    own = inc(V.quantize_mx(T.ec[:, OT:OP], T.es[:, OT:OP], T.eb[:]), "v")
 
     far = topo.engines(core, who["diag"])
-    near = topo.engines(core, who["partner"])
-    inner = [e for e in near if e not in far]
-    h = len(far) // 2
-    LEAD, TRAIL = O0, O0 + SL
+    inner = inner_engines(core, who, topo)
+    h, hi = len(far) // 2, len(inner) // 2
 
-    def early(s):
-        return [(helper, inner[:HE], OP, 0, s)]
+    def plane(es, s):
+        return (who["plane"], es, SRC[side], P1 + RUN * side, s)
 
-    def first(s):
-        return [(who["plane"], far[:h], LEAD, P1, s), (who["diag"], far[h:], TRAIL, P1 + RUN, s), (who["partner"], inner, LEAD, TP, sem.ap)]
+    def diag(es, s):
+        return (who["diag"], es, SRC[1 - side], P1 + RUN * (1 - side), s)
 
-    second = [(who["mate_a"], far[:h], LEAD, P2, sem.a2), (who["mate_b"], far[h:], TRAIL, P2 + RUN, sem.a2)]
-    relay = [(who["partner"], inner, P1 + SL, P3, sem.a3)]
+    def partner(es):
+        return (who["partner"], es, SRC[side], TP + SL * side, sem.ap)
+
+    def relay(es):
+        return [(who["partner"], es, P1 + SL, P3, sem.a3)]
 
     def snd(items, n, codes):
         return send(g, core, T, topo, items, n, codes)
 
-    g.wait_ge(sem.v, hq)
-    sent = snd(early(sem.hc), SL, True)
+    g.wait_ge(sem.v, hq[side])
+    sent = snd([(helper, inner, PL[side], HP, sem.hc)], SL, True)
     g.wait_ge(sem.v, own)
-    sent += snd(first(sem.a1c), RUN, True)
-    sent += snd(early(sem.hs), SL, False)
-    sent += snd(first(sem.a1s), RUN, False)
-    sent += snd(second, RUN, True)
-    sent += snd(second, RUN, False)
+    sent += snd([plane(far, sem.a0c), partner(inner)], RUN, True)
+    sent += snd([plane(far, sem.a0s), partner(inner[:hi]), (helper, inner[hi:], SRC[side], SRC[side], sem.hs)], RUN, False)
+    sent += snd([diag(far, sem.a1c)], RUN, True)
+    sent += snd([diag(far, sem.a1s)], RUN, False)
+    sent += snd(halves(core, [who["mate_a"], who["mate_b"]], SRC[side], [P2 + RUN * side] * 2, sem.a2, topo), RUN, True)
+    ends1 = (P1, Z2 - SL)
+    for codes, s in ((True, sem.a0c), (False, sem.a0s)):
+        g.wait_ge(s, len(far))
+        sent += snd([(who["partner"], inner, ends1[side], HP, sem.ah)], SL, codes)
     g.wait_ge(sem.a1c, len(far))
-    sent += snd(relay, 2 * K, True)
+    sent += snd(relay(inner), 2 * K, True)
     g.wait_ge(sem.a1s, len(far))
-    sent += snd(relay, 2 * K, False)
+    sent += snd(relay(inner), 2 * K, False)
 
     V.wait_ge(sem.lx, 16)
     S.wait_ge(sem.lx, 16)
     vx = inc(V.tensor_copy(T.xr[:, :, 0:4 * G], T.xs[:, :, :]), "v")
     sx = inc(S.activation(T.xr[:, :, 4 * G:4 * B], T.xs[:, :, :], COPY), "s")
-    V.wait_ge(sem.lq, 16)
-    qq = inc(V.quantize_mx(T.qc[:], T.qp[:], T.qb[:]), "v")
+    inc(V.quantize_mx(T.ec[:, Z3:P3], T.es[:, Z3:P3], T.hb[:, 0:4 * NH]), "v")
     V.wait_ge(sem.v, vx)
     V.wait_ge(sem.s, sx)
     xq = inc(V.quantize_mx(T.xc[:], T.xp[:], T.xr[:, :, :]), "v")
-    for c in (Z1, Z2, Z3):
-        zq = inc(V.quantize_mx(T.ec[:, c:c + NH], T.es[:, c:c + NH], T.hb[:, 4 * SL:4 * (SL + NH)]), "v")
+    V.wait_ge(sem.lq, 16)
+    qq = inc(V.quantize_mx(T.qc[:], T.qp[:], T.qb[:]), "v")
 
-    hfree, tfree, nt, nh, trfree = [0] * HBANKS, [None] * TBANKS, [0], [0], [0]
+    hfree, tfree, nt, nh = [0] * HBANKS, [None] * TBANKS, [0], [0]
+    ROW = (NH - SL, 0)
 
-    def planes(c, start, stop):
+    def planes(c, s, start, stop):
         b = nh[0] % HBANKS
         if start and hfree[b]:
             PE.wait_ge(sem.v, hfree[b])
+        c -= ROW[s]
         return inc(PE.matmul_mx(T.hps[:, 512 * b:512 * b + XW], T.ec[:, c:c + NH], T.es[:, c:c + NH], T.xc[:], T.xp[:], start, stop), "t")
 
-    def at(k):
-        return BW * (k // 4) + LW * (k % 4)
-
-    def lists(t, rows):
+    def turn(t):
         b = nh[0] % HBANKS
         nh[0] += 1
         V.wait_ge(sem.t, t)
-        n = hfree[b] = inc(V.transpose(T.tr[:, :, :], T.hps[:, 512 * b:512 * b + XW]), "v")
-        V.wait_ge(sem.v, n)
+        hfree[b] = inc(V.transpose(T.tr[:, A * b:A * (b + 1), :], T.hps[:, 512 * b:512 * b + XW]), "v")
+        return b
+
+    def signs(b, rows):
+        V.wait_ge(sem.v, hfree[b])
         for name, row in rows.items():
-            p, i, d = row // B * B, row % B, at(slot[name])
-            n = inc(V.tensor_scalar(T.bits[0:B, d:d + LW], T.tr[p:p + B, :, i:i + SL], 0.0, float(2 ** (NBIT - 1)),
+            p, i, d = row // B * B, row % B, at[name]
+            n = inc(V.tensor_scalar(T.bits[0:B, d:d + LW], T.tr[p:p + B, A * b:A * (b + 1), i:i + SL], 0.0, float(2 ** (NBIT - 1)),
                                     AluOpType.is_gt, AluOpType.mult), "v")
-        ks = sorted(slot[name] for name in rows)
-        lo, w = at(ks[0]), LW * len(ks)
+        return n
+
+    def lists(n, names):
+        lo, hi = min(at[name] for name in names), max(at[name] for name in names) + LW
         V.wait_ge(sem.v, n)
-        n = inc(V.tensor_tensor_scan(T.bsum[0:B, lo:lo + w], T.half[0:B, 0:w], T.bits[0:B, lo:lo + w], 0.0, AluOpType.mult, AluOpType.add), "v")
+        n = inc(V.tensor_tensor_scan(T.bsum[0:B, lo:hi], T.half[0:B, 0:hi - lo], T.bits[0:B, lo:hi], 0.0, AluOpType.mult, AluOpType.add), "v")
         V.wait_ge(sem.v, n)
         for p in range(0, 128, B):
-            n = inc(V.tensor_copy(T.offs[p:p + B, A * ks[0]:A * (ks[-1] + 1)], T.bsum[0:B, lo + NBIT - 1:lo + w:SL]), "v")
+            n = inc(V.tensor_copy(T.offs[p:p + B, lo // SL:hi // SL], T.bsum[0:B, lo + NBIT - 1:hi:SL]), "v")
         return n
 
     ready, where, used = {}, {}, [0]
@@ -235,67 +270,81 @@ def rank_program(g, core, T, topo):
     nst = {"st": 0, "sst": 0}
     picked = {}
 
-    def pick(names, o, made):
-        E = S if o else V
-        E.wait_ge(sem.v, made)
-        E.wait_ge(sem.s, max(ready[name, o] for name in names))
-        for name in names:
-            j, c, k = q_of[name] * O + o, where[name, o], slot[name]
-            out, win = T.ys[:, T_TOK * j:T_TOK * (j + 1)], T.prod[:, c:c + K].indirect(T.offs[:, A * k:A * (k + 1)])
-            picked[name, o] = inc(S.activation(out, win, COPY), "s") if o else inc(V.tensor_copy(out, win), "v")
+    def pick(name, made, on="vs"):
+        for o, n in enumerate(on):
+            E = V if n == "v" else S
+            E.wait_ge(sem.v, made)
+            E.wait_ge(sem.s, ready[name, o])
+            j, c, k = q_of[name] * O + o, where[name, o], at[name] // SL
+            out, win = T.ys[:, T_TOK * j:T_TOK * (j + 1)], T.prod[:, c:c + K].indirect(T.offs[:, k:k + A])
+            picked[name, o] = (sem[n], inc(V.tensor_copy(out, win) if n == "v" else S.activation(out, win, COPY), n))
 
     def store(names):
-        w = O * T_TOK
+        lo, hi = O * T_TOK * min(q_of[n] for n in names), O * T_TOK * (max(q_of[n] for n in names) + 1)
         for name in names:
-            q = q_of[name]
-            Y.wait_ge(sem.v, picked[name, 0])
-            Y.wait_ge(sem.s, picked[name, 1])
-            Y.dma_start(T.y[:, w * q:w * (q + 1)], T.ys[:, w * q:w * (q + 1)]).then_inc(sem.st, 16)
-            nst["st"] += 16
+            for o in range(O):
+                Y.wait_ge(*picked[name, o])
+        Y.dma_start(T.y[:, lo:hi], T.ys[:, lo:hi]).then_inc(sem.st, 16)
+        nst["st"] += 16
 
-    def buckets(b, D, dsem):
+    def buckets(b, names):
         n = inc(V.transpose(T.bt[0:B, B * b:B * (b + 1)], T.bsum[0:B, BW * b + NBIT - 1:BW * (b + 1):SL]), "v")
-        D.wait_ge(sem.v, n)
-        for i in range(2):
-            q0, q1 = (q_of[name] for name in twos[2 * b + i])
-            D.dma_start(T.bk[q0:q1 + 1:q1 - q0, :], T.bt[2 * A * i:2 * A * (i + 1), B * b:B * b + G]).then_inc(sem[dsem], 16)
-            nst[dsem] += 16
 
-    BEFORE = SL - NH
-    PE.wait_ge(sem.v, qq)
-    tables(TRAIL, ["own"])
+        def rows(k, w):
+            def issue(D, dsem):
+                q = q_of[names[k]]
+                D.wait_ge(sem.v, n)
+                D.dma_start(T.bk[q:q + w, :], T.bt[A * k:A * (k + w), B * b:B * b + G]).then_inc(sem[dsem], 16)
+                nst[dsem] += 16
+            return issue
+
+        starts = [k for k in range(len(names)) if k == 0 or q_of[names[k]] != q_of[names[k - 1]] + 1]
+        return [rows(k, e - k) for k, e in zip(starts, starts[1:] + [len(names)])]
+
     PE.wait_ge(sem.v, xq)
-    planes(OP, True, False)
-    PE.wait_ge(sem.ap, 2 * len(inner))
-    l0 = lists(planes(TP + BEFORE, False, True), {"own": 0, "partner": NH - SL})
-    tables(TP + SL, ["partner"])
-    for o in range(O):
-        pick(["own", "partner"], o, l0)
-    store(["own", "partner"])
+    t0 = planes(OP, 1, True, True)
+    PE.wait_ge(sem.v, qq)
+    l0 = lists(signs(turn(t0), {"own": 0}), ["own"])
+    tables(OT, ["own"])
+    pick("own", l0)
+    for b, names in enumerate((early, late)):
+        inc(V.memset(T.bsum[0:B, BW * b + LW * len(names):BW * (b + 1)], 0.0), "v")
 
-    PE.wait_ge(sem.v, zq)
+    other = 1 - side
+    PE.wait_ge(sem.ap, len(inner) + hi)
+    planes(TP + RUN * other, other, True, False)
+    tables(TP + SL, ["partner"])
+    PE.wait_ge(sem.a0c, len(far))
+    PE.wait_ge(sem.a0s, len(far))
+    l1 = lists(signs(turn(planes(ends1[side], side, False, True)), {"partner": ROW[other], "plane": ROW[side]}), ["partner", "plane"])
+    tables(P1 + SL + K * side, ["plane"])
+
     PE.wait_ge(sem.a1c, len(far))
     PE.wait_ge(sem.a1s, len(far))
-    planes(P1 + BEFORE, True, False)
-    l1 = lists(planes(Z2 - SL, False, True), {"plane": NH - SL, "diag": 0})
-    tables(P1 + SL, ["plane", "diag"])
-    for o in range(O):
-        pick(["plane", "diag"], o, l1)
-    store(["plane", "diag"])
-    buckets(0, Y, "st")
+    td = planes(ends1[other], other, True, True)
+    tables(P1 + SL + K * other, ["diag"])
+    for row in buckets(0, early):
+        row(Y, "st")
+    pick("plane", l1)
+    store(["plane"])
+    pick("partner", l1, "ss")
+    store(["own", "partner"])
+    bd = turn(td)
 
     PE.wait_ge(sem.a2, 2 * len(far))
-    PE.wait_ge(sem.ah, 2 * len(far))
-    planes(P2 + BEFORE, True, False)
-    l2 = lists(planes(HP - SL, False, True), {"mate_a": NH - SL, "mate_b": 0, "plane_o": SL, "diag_o": 2 * SL})
-    tables(P2 + SL, ["mate_a", "mate_b"])
+    planes(P2, 0, True, False)
+    PE.wait_ge(sem.ah, 2 * len(far) + 2 * len(inner))
+    bl = turn(planes(HP - SL, 1, False, True))
+    signs(bd, {"diag": ROW[other]})
+    l2 = lists(signs(bl, {pair2[0]: ROW[0], pair2[1]: 0, "plane_o": SL, "diag_o": 2 * SL}), late)
+    for row in buckets(1, late):
+        row(Y, "st")
+    tables(P2 + SL, pair2)
     PE.wait_ge(sem.a3, 2 * len(inner))
-    tables(P3, ["plane_o", "diag_o"])
-    pick(["mate_a", "mate_b"], 0, l2)
-    pick(["plane_o", "diag_o"], 0, l2)
-    pick(["mate_a", "mate_b", "plane_o", "diag_o"], 1, l2)
-    store(["mate_a", "mate_b", "plane_o", "diag_o"])
-    buckets(1, S, "sst")
+    tables(P3, pair3)
+    for name in ["diag"] + pair2 + pair3:
+        pick(name, l2)
+        store([name])
 
     g.wait_ge(sem.sent, sent)
     g.wait_ge(sem.v, cnt["v"])

from concourse.bass import DstId, RemoteDMATransfer
from concourse.mybir import dt, AluOpType, ActivationFunctionType

T_TOK, NBIT, K, O, N = 96, 7, 128, 2, 8
G = 16
B = 32
A = T_TOK // G
SL = 8
RUN = K + SL
NH = 128
XW = A * B
OT = NH
OP = OT + K
TP = OP + NH
Z1 = TP + RUN + SL
P1 = Z1 + NH
Z2 = P1 + 2 * RUN
P2 = Z2 + NH
HP = P2 + 2 * RUN
Z3 = HP + 2 * SL
P3 = Z3 + NH
COLS = P3 + 2 * K
SRC = (OT - SL, OT)
PL = (OT - SL, OP)
HBANKS, TBANKS = 2, 6
LW = A * SL
BW = B * SL

SCRATCH = {
    "hb": ("sbuf", [128, 4 * (2 * NH + SL)], "bfloat16"),
    "eb": ("sbuf", [128, 4 * K], "bfloat16"),
    "xs": ("sbuf", [128, A, 4 * G], "bfloat16"),
    "xr": ("sbuf", [128, A, 4 * B], "bfloat16"),
    "qb": ("sbuf", [128, O * 512], "bfloat16"),
    "ec": ("sbuf", [128, COLS], "float8_e4m3fn_x4"),
    "es": ("sbuf", [128, COLS], "uint8"),
    "xc": ("sbuf", [128, XW], "float8_e4m3fn_x4"),
    "xp": ("sbuf", [128, XW], "uint8"),
    "qc": ("sbuf", [128, O * 128], "float8_e4m3fn_x4"),
    "qp": ("sbuf", [128, O * 128], "uint8"),
    "tr": ("sbuf", [128, HBANKS * A, B], "float32"),
    "bits": ("sbuf", [128, 2 * BW], "bfloat16"),
    "half": ("sbuf", [128, BW], "bfloat16"),
    "bsum": ("sbuf", [128, 2 * BW], "float32"),
    "offs": ("sbuf", [128, 2 * B], "uint16"),
    "bt": ("sbuf", [128, 2 * B], "float32"),
    "prod": ("sbuf", [128, N * O * K], "float32"),
    "ys": ("sbuf", [128, N * O * T_TOK], "float32"),
    "hps": ("psum", [128, 512 * HBANKS], "float32"),
    "tps": ("psum", [128, 512 * TBANKS], "float32"),
}
SEMAPHORES = ["le", "lh", "lx", "lq", "v", "s", "t", "ah", "hc", "hs", "ap", "a0c", "a1c", "a0s", "a1s", "a2", "a3", "sent", "st", "sst"]


def roles(core, T, topo):
    who = {"own": core}
    for d in T.cores:
        if d == core:
            continue
        same = topo.die(d) == topo.die(core)
        if d in topo.cores_of(core):
            who["partner"] = d
        elif topo.mates(core, d):
            who["mate_a" if same else "mate_b"] = d
        elif topo.same_plane(core, d):
            who["plane" if same else "plane_o"] = d
        else:
            who["diag" if same else "diag_o"] = d
    return who


def transfer(core, T, topo, item, n, codes):
    d, es, c0, c1, s = item
    rid, pid = topo.addr(d, core)
    buf = T.ec if codes else T.es
    src, dst = buf[:, c0:c0 + n], buf[:, c1:c1 + n]
    if codes:
        src, dst = src.bitcast(dt.uint8), dst.bitcast(dt.uint8)
    return RemoteDMATransfer(dst_ids=[DstId(rid=rid, pnc=pid)], dma_engine_mask=sum(1 << e for e in es), remote_sem=s, src=src, dst=dst)


def send(g, core, T, topo, items, n, codes):
    g.remote_dma_fused([transfer(core, T, topo, i, n, codes) for i in items], local_sem=T.sem.sent)
    return sum(len(i[1]) for i in items)


def halves(core, dests, c0, cols, s, topo):
    items = []
    for i, (d, c1) in enumerate(zip(dests, cols)):
        es = topo.engines(core, d)
        n = len(es) // 2
        items.append((d, es[n * i:n * (i + 1)], c0, c1, s))
    return items


def inner_engines(core, who, topo):
    far = topo.engines(core, who["diag"])
    return [e for e in topo.engines(core, who["partner"]) if e not in far]


def helper_program(g, core, r, T, topo):
    who, side = roles(r, T, topo), topo.die(r)
    codes, planes = ([(who["diag_o"], topo.engines(core, who["diag_o"]), c, HP + SL, T.sem.ah)] for c in (HP, PL[side]))
    mates = halves(core, [who["mate_a"], who["mate_b"]], SRC[side], [P2 + RUN * side] * 2, T.sem.a2, topo)
    n = len(inner_engines(r, who, topo))
    g.wait_ge(T.sem.hc, n)
    sent = send(g, core, T, topo, codes, SL, True)
    g.wait_ge(T.sem.hs, n // 2)
    sent += send(g, core, T, topo, planes, SL, False)
    sent += send(g, core, T, topo, mates, RUN, False)
    g.wait_ge(T.sem.sent, sent)


def rank_program(g, core, T, topo):
    sem = T.sem
    helper = None
    for r in T.cores:
        if core not in topo.cores_of(r):
            continue
        dests = [d for d in T.cores if d not in topo.cores_of(r)]
        spare = [c for c in topo.cores_of(r) if c not in T.cores and topo.die(c) == topo.die(r) and all(topo.may_write(c, d) for d in dests)]
        if core == spare[0]:
            helper_program(g, core, r, T, topo)
        if core == r:
            helper = spare[0]
    rank = T.rank_of(core)
    if rank is None:
        return
    who, side = roles(core, T, topo), topo.die(core)
    q_of = {n: T.rank_of(d) for n, d in who.items()}
    early = ["own", "partner", "plane"]
    late = sorted((n for n in who if n not in early), key=lambda n: q_of[n])
    at = {n: BW * b + LW * k for b, names in enumerate((early, late)) for k, n in enumerate(names)}

    def by_side(same, other):
        return [other, same] if side else [same, other]

    pair1, pair2, pair3 = by_side("plane", "diag"), by_side("mate_a", "mate_b"), by_side("diag_o", "plane_o")

    cnt = {"v": 0, "s": 0, "t": 0}

    def inc(call, name):
        call.then_inc(sem[name], 1)
        cnt[name] += 1
        return cnt[name]

    V, S, PE, Y = g.vector, g.scalar, g.tensor, g.sync
    COPY = ActivationFunctionType.Copy

    S.dma_start(T.hb[:, 4 * NH:4 * (NH + SL)], T.hp[:, 0:4 * SL]).then_inc(sem.lh, 16)
    Y.dma_start(T.eb[:], T.e[:]).then_inc(sem.le, 16)
    Y.dma_start(T.xs[:], T.x[:]).then_inc(sem.lx, 16)
    Y.dma_start(T.qb[:], T.qw[:]).then_inc(sem.lq, 16)

    z = inc(V.memset(T.hb[:, 0:4 * NH], 0.0), "v")
    inc(V.memset(T.hb[:, 4 * (NH + SL):], 0.0), "v")
    m = inc(V.memset(T.half[0:B, :], 0.5), "v")
    V.wait_ge(sem.v, z)
    for c in (Z1, Z2):
        inc(V.quantize_mx(T.ec[:, c:c + NH], T.es[:, c:c + NH], T.hb[:, 0:4 * NH]), "v")
    V.wait_ge(sem.v, m)
    inc(V.memset(T.half[0:B, 0:BW:SL], 0.0), "v")

    V.wait_ge(sem.lh, 16)
    hq = {}
    for s in (side, 1 - side):
        c, h = (OP, 4 * NH) if s else (0, 4 * SL)
        hq[s] = inc(V.quantize_mx(T.ec[:, c:c + NH], T.es[:, c:c + NH], T.hb[:, h:h + 4 * NH]), "v")
    V.wait_ge(sem.le, 16)
    own = inc(V.quantize_mx(T.ec[:, OT:OP], T.es[:, OT:OP], T.eb[:]), "v")

    far = topo.engines(core, who["diag"])
    inner = inner_engines(core, who, topo)
    h, hi = len(far) // 2, len(inner) // 2

    def plane(es, s):
        return (who["plane"], es, SRC[side], P1 + RUN * side, s)

    def diag(es, s):
        return (who["diag"], es, SRC[1 - side], P1 + RUN * (1 - side), s)

    def partner(es):
        return (who["partner"], es, SRC[side], TP + SL * side, sem.ap)

    def relay(es):
        return [(who["partner"], es, P1 + SL, P3, sem.a3)]

    def snd(items, n, codes):
        return send(g, core, T, topo, items, n, codes)

    g.wait_ge(sem.v, hq[side])
    sent = snd([(helper, inner, PL[side], HP, sem.hc)], SL, True)
    g.wait_ge(sem.v, own)
    sent += snd([plane(far, sem.a0c), partner(inner)], RUN, True)
    sent += snd([plane(far, sem.a0s), partner(inner[:hi]), (helper, inner[hi:], SRC[side], SRC[side], sem.hs)], RUN, False)
    sent += snd([diag(far, sem.a1c)], RUN, True)
    sent += snd([diag(far, sem.a1s)], RUN, False)
    sent += snd(halves(core, [who["mate_a"], who["mate_b"]], SRC[side], [P2 + RUN * side] * 2, sem.a2, topo), RUN, True)
    ends1 = (P1, Z2 - SL)
    for codes, s in ((True, sem.a0c), (False, sem.a0s)):
        g.wait_ge(s, len(far))
        sent += snd([(who["partner"], inner, ends1[side], HP, sem.ah)], SL, codes)
    g.wait_ge(sem.a1c, len(far))
    sent += snd(relay(inner), 2 * K, True)
    g.wait_ge(sem.a1s, len(far))
    sent += snd(relay(inner), 2 * K, False)

    V.wait_ge(sem.lx, 16)
    S.wait_ge(sem.lx, 16)
    vx = inc(V.tensor_copy(T.xr[:, :, 0:4 * G], T.xs[:, :, :]), "v")
    sx = inc(S.activation(T.xr[:, :, 4 * G:4 * B], T.xs[:, :, :], COPY), "s")
    inc(V.quantize_mx(T.ec[:, Z3:P3], T.es[:, Z3:P3], T.hb[:, 0:4 * NH]), "v")
    V.wait_ge(sem.v, vx)
    V.wait_ge(sem.s, sx)
    xq = inc(V.quantize_mx(T.xc[:], T.xp[:], T.xr[:, :, :]), "v")
    V.wait_ge(sem.lq, 16)
    qq = inc(V.quantize_mx(T.qc[:], T.qp[:], T.qb[:]), "v")

    hfree, tfree, nt, nh = [0] * HBANKS, [None] * TBANKS, [0], [0]
    ROW = (NH - SL, 0)

    def planes(c, s, start, stop):
        b = nh[0] % HBANKS
        if start and hfree[b]:
            PE.wait_ge(sem.v, hfree[b])
        c -= ROW[s]
        return inc(PE.matmul_mx(T.hps[:, 512 * b:512 * b + XW], T.ec[:, c:c + NH], T.es[:, c:c + NH], T.xc[:], T.xp[:], start, stop), "t")

    def turn(t):
        b = nh[0] % HBANKS
        nh[0] += 1
        V.wait_ge(sem.t, t)
        hfree[b] = inc(V.transpose(T.tr[:, A * b:A * (b + 1), :], T.hps[:, 512 * b:512 * b + XW]), "v")
        return b

    def signs(b, rows):
        V.wait_ge(sem.v, hfree[b])
        for name, row in rows.items():
            p, i, d = row // B * B, row % B, at[name]
            n = inc(V.tensor_scalar(T.bits[0:B, d:d + LW], T.tr[p:p + B, A * b:A * (b + 1), i:i + SL], 0.0, float(2 ** (NBIT - 1)),
                                    AluOpType.is_gt, AluOpType.mult), "v")
        return n

    def lists(n, names):
        lo, hi = min(at[name] for name in names), max(at[name] for name in names) + LW
        V.wait_ge(sem.v, n)
        n = inc(V.tensor_tensor_scan(T.bsum[0:B, lo:hi], T.half[0:B, 0:hi - lo], T.bits[0:B, lo:hi], 0.0, AluOpType.mult, AluOpType.add), "v")
        V.wait_ge(sem.v, n)
        for p in range(0, 128, B):
            n = inc(V.tensor_copy(T.offs[p:p + B, lo // SL:hi // SL], T.bsum[0:B, lo + NBIT - 1:hi:SL]), "v")
        return n

    ready, where, used = {}, {}, [0]

    def tables(c, names):
        w = K * len(names)
        for o in range(O):
            i = nt[0] % TBANKS
            nt[0] += 1
            if tfree[i]:
                PE.wait_ge(sem.s, tfree[i])
            t = inc(PE.matmul_mx(T.tps[:, 512 * i:512 * i + w], T.qc[:, 128 * o:128 * (o + 1)], T.qp[:, 128 * o:128 * (o + 1)],
                                 T.ec[:, c:c + w], T.es[:, c:c + w], True, True), "t")
            S.wait_ge(sem.t, t)
            tfree[i] = inc(S.activation(T.prod[:, used[0]:used[0] + w], T.tps[:, 512 * i:512 * i + w], COPY), "s")
            for j, name in enumerate(names):
                ready[name, o], where[name, o] = tfree[i], used[0] + K * j
            used[0] += w

    nst = {"st": 0, "sst": 0}
    picked = {}

    def pick(name, made, on="vs"):
        for o, n in enumerate(on):
            E = V if n == "v" else S
            E.wait_ge(sem.v, made)
            E.wait_ge(sem.s, ready[name, o])
            j, c, k = q_of[name] * O + o, where[name, o], at[name] // SL
            out, win = T.ys[:, T_TOK * j:T_TOK * (j + 1)], T.prod[:, c:c + K].indirect(T.offs[:, k:k + A])
            picked[name, o] = (sem[n], inc(V.tensor_copy(out, win) if n == "v" else S.activation(out, win, COPY), n))

    def store(names):
        lo, hi = O * T_TOK * min(q_of[n] for n in names), O * T_TOK * (max(q_of[n] for n in names) + 1)
        for name in names:
            for o in range(O):
                Y.wait_ge(*picked[name, o])
        Y.dma_start(T.y[:, lo:hi], T.ys[:, lo:hi]).then_inc(sem.st, 16)
        nst["st"] += 16

    def buckets(b, names):
        n = inc(V.transpose(T.bt[0:B, B * b:B * (b + 1)], T.bsum[0:B, BW * b + NBIT - 1:BW * (b + 1):SL]), "v")

        def rows(k, w):
            def issue(D, dsem):
                q = q_of[names[k]]
                D.wait_ge(sem.v, n)
                D.dma_start(T.bk[q:q + w, :], T.bt[A * k:A * (k + w), B * b:B * b + G]).then_inc(sem[dsem], 16)
                nst[dsem] += 16
            return issue

        starts = [k for k in range(len(names)) if k == 0 or q_of[names[k]] != q_of[names[k - 1]] + 1]
        return [rows(k, e - k) for k, e in zip(starts, starts[1:] + [len(names)])]

    PE.wait_ge(sem.v, xq)
    t0 = planes(OP, 1, True, True)
    PE.wait_ge(sem.v, qq)
    l0 = lists(signs(turn(t0), {"own": 0}), ["own"])
    tables(OT, ["own"])
    pick("own", l0)
    for b, names in enumerate((early, late)):
        inc(V.memset(T.bsum[0:B, BW * b + LW * len(names):BW * (b + 1)], 0.0), "v")

    other = 1 - side
    PE.wait_ge(sem.ap, len(inner) + hi)
    planes(TP + RUN * other, other, True, False)
    tables(TP + SL, ["partner"])
    PE.wait_ge(sem.a0c, len(far))
    PE.wait_ge(sem.a0s, len(far))
    l1 = lists(signs(turn(planes(ends1[side], side, False, True)), {"partner": ROW[other], "plane": ROW[side]}), ["partner", "plane"])
    tables(P1 + SL + K * side, ["plane"])

    PE.wait_ge(sem.a1c, len(far))
    PE.wait_ge(sem.a1s, len(far))
    td = planes(ends1[other], other, True, True)
    tables(P1 + SL + K * other, ["diag"])
    for row in buckets(0, early):
        row(Y, "st")
    pick("plane", l1)
    store(["plane"])
    pick("partner", l1, "ss")
    store(["own", "partner"])
    bd = turn(td)

    PE.wait_ge(sem.a2, 2 * len(far))
    planes(P2, 0, True, False)
    PE.wait_ge(sem.ah, 2 * len(far) + 2 * len(inner))
    bl = turn(planes(HP - SL, 1, False, True))
    signs(bd, {"diag": ROW[other]})
    l2 = lists(signs(bl, {pair2[0]: ROW[0], pair2[1]: 0, "plane_o": SL, "diag_o": 2 * SL}), late)
    for row in buckets(1, late):
        row(Y, "st")
    tables(P2 + SL, pair2)
    PE.wait_ge(sem.a3, 2 * len(inner))
    tables(P3, pair3)
    for name in ["diag"] + pair2 + pair3:
        pick(name, l2)
        store([name])

    g.wait_ge(sem.sent, sent)
    g.wait_ge(sem.v, cnt["v"])
    g.wait_ge(sem.s, cnt["s"])
    g.wait_ge(sem.t, cnt["t"])
    S.wait_ge(sem.sst, nst["sst"])
    Y.wait_ge(sem.st, nst["st"])
